import numpy as np
import ml_dtypes


def mxq(x, axis, fmt="e4m3"):
    dtype, down = {"e4m3": (ml_dtypes.float8_e4m3fn, 7), "e5m2": (ml_dtypes.float8_e5m2, 14)}[fmt]
    v = np.moveaxis(np.asarray(x, np.float32).astype(ml_dtypes.bfloat16).astype(np.float64), axis, -1)
    blocks = v.reshape(v.shape[:-1] + (-1, 32))
    amax = np.abs(blocks).max(-1, keepdims=True)
    byte = np.maximum(np.where(amax > 0, np.frexp(amax)[1] - 1 + 127, 0) - down, 1)
    scale = np.exp2(byte - 127.0)
    codes = (blocks / scale).astype(np.float32).astype(dtype).astype(np.float64)
    return np.moveaxis((codes * scale).reshape(v.shape), -1, axis)


WIDE = False


def mx_kscale(k):
    if not WIDE:
        return np.ones(k)
    levels = np.array([10, -10, 5, -5, 0])
    if k % 512:
        return np.exp2(np.random.permutation(np.resize(levels, k // 32))).repeat(32)
    a = np.empty((k // 512, 16))
    for p in range(k // 512):
        a[p, :8] = np.random.permutation(np.resize(levels, 8))
        for g in range(8):
            far = levels[np.abs(levels - a[p, g]) >= 10]
            a[p, g + 8] = far[np.random.randint(len(far))]
    return np.exp2(a.ravel()).repeat(32)


def f64(x):
    return np.asarray(x).astype(np.float64)


E2M1 = np.array([0.0, 0.5, 1.0, 1.5, 2.0, 3.0, 4.0, 6.0, -0.0, -0.5, -1.0, -1.5, -2.0, -3.0, -4.0, -6.0])


def pack_weight(w, fmt):
    k, n = w.shape
    w = f64(np.asarray(w, np.float32).astype(ml_dtypes.bfloat16)).reshape(k // 32, 32, n)
    amax = np.abs(w).max(1)
    if fmt == "e4m3":
        byte = np.frexp(amax)[1] - 1 + 127 - 7
    else:
        mant, ex = np.frexp(amax / 6.0)
        byte = np.where(mant > 0.5, ex, ex - 1) + 127
    byte = np.clip(np.where(amax > 0, byte, 1), 1, 254)
    scaled = (w * np.exp2(127.0 - byte)[:, None, :]).reshape(k, n).astype(np.float32)
    by_word = np.ascontiguousarray(scaled.reshape(k // 512, 128, 4, n).transpose(0, 1, 3, 2))
    if fmt == "e4m3":
        words = by_word.astype(ml_dtypes.float8_e4m3fn).view(np.uint8)
    else:
        c = by_word.astype(ml_dtypes.float4_e2m1fn).view(np.uint8) & 0xF
        words = (c[..., 0::2] | (c[..., 1::2] << 4)).reshape(k // 512, 128, 2 * n)
    return np.ascontiguousarray(words), np.ascontiguousarray(byte.astype(np.uint8).reshape(k // 512, 16, n))


def unpack_weight(words, scales, fmt):
    g, _, n = scales.shape
    words = np.ascontiguousarray(words).reshape(g, 128, n, -1)
    if fmt == "e4m3":
        vals = words.view(ml_dtypes.float8_e4m3fn).astype(np.float64)
    else:
        nib = np.empty((g, 128, n, 4), np.uint8)
        nib[..., 0::2] = words & 0xF
        nib[..., 1::2] = words >> 4
        vals = E2M1[nib]
    vals = vals * np.repeat(np.exp2(scales.astype(np.float64) - 127.0), 8, axis=1)[..., None]
    return vals.transpose(0, 1, 3, 2).reshape(g * 512, n)


def planes(y):
    n, m = y.shape
    v = y.astype(np.float32).astype(ml_dtypes.bfloat16).astype(np.float64).reshape(n // 32, 32, m)
    top = np.abs(v).max(1)
    byte = np.clip(np.where(top > 0, np.frexp(top)[1] - 1 + 127 - 7, 1), 1, 254)
    codes = (v * np.exp2(127.0 - byte)[:, None, :]).reshape(n, m).astype(np.float32).astype(ml_dtypes.float8_e4m3fn).view(np.uint8)
    words = codes.reshape(n // 512, 128, 4, m).transpose(0, 1, 3, 2)
    return np.ascontiguousarray(words), np.ascontiguousarray(byte.astype(np.uint8).reshape(n // 512, 16, m))


K, M, T = 1536, 1024, 512


def setup_inputs():
    n = np.random.standard_normal
    s = mx_kscale(K)[:, None]
    x = n((K, T)) * s
    x4 = pack_weight(x, "e2m1")
    rest = x - unpack_weight(*x4, "e2m1")
    p_w4 = pack_weight(n((K, M)) / np.sqrt(K) / s, "e2m1")
    return {
        "x4_words": x4[0],
        "x4_scales": x4[1],
        "xr": (rest).astype(np.float32),
        "w4_words": p_w4[0],
        "w4_scales": p_w4[1],
    }


def reference(x4_words, x4_scales, xr, w4_words, w4_scales):
    x4_ = unpack_weight(x4_words, x4_scales, "e2m1")
    xr_ = mxq(f64(xr), 0, "e4m3")
    w4_ = unpack_weight(w4_words, w4_scales, "e2m1")
    y = x4_.T @ w4_ + xr_.T @ w4_
    out_0 = y
    return (out_0,) + planes(out_0)

@@ -1,0 +1,201 @@
+from contextlib import ExitStack
+
+import concourse.mybir as mybir
+
+K, M, T = 1536, 1024, 512
+FLOPS = 2 * 2 * K * M * T
+
+F32 = mybir.dt.float32
+BF16 = mybir.dt.bfloat16
+I32 = mybir.dt.int32
+U32 = mybir.dt.uint32
+U8 = mybir.dt.uint8
+FP8X4 = mybir.dt.float8_e4m3fn_x4
+FP4X4 = mybir.dt.float4_e2m1fn_x4
+
+P = 128
+PACK = 4
+PASSES = K // (P * PACK)
+N_TILE = 512
+HALVES = M // N_TILE
+QUADS = 4
+
+
+def tile_mix_xres_tm_pl_none_kernel(
+    tc, x4_words, x4_scales, xr, w4_words, w4_scales, out_0, out_1, out_2
+):
+    nc = tc.nc
+    with ExitStack() as ctx:
+        sb = ctx.enter_context(tc.tile_pool(name="sb", bufs=1))
+        psum = ctx.enter_context(tc.psum_pool(name="psum", bufs=1))
+        ctx.enter_context(tc.manual_schedule())
+
+        def sbuf(name, shape, dtype):
+            return sb.tile(shape, dtype, name=name, align_bytes=64)
+
+        xs_raw = sbuf("xs_raw", [P, PASSES, T], U8)
+        ws = sbuf("ws", [P, PASSES, M], U8)
+        xw_first = sbuf("xw_first", [P, 2 * T], U8)
+        xw_rest = sbuf("xw_rest", [P, PASSES - 1, 2 * T], U8)
+        xw_raw = [xw_first[:]] + [xw_rest[:, a, :] for a in range(PASSES - 1)]
+        ww = [sbuf("ww%d" % a, [P, 2 * M], U8) for a in range(PASSES)]
+        xw = [sbuf("xw%d" % a, [P, PACK, 2 * P], U8) for a in range(PASSES)]
+        xs = [sbuf("xs%d" % a, [P, PACK, P], U8) for a in range(PASSES)]
+        xr_raw = [sbuf("xr_raw%d" % a, [P, PACK, T], F32) for a in range(PASSES)]
+        xr_bf = [[sbuf("xr_bf%d_%d" % (a, u), [P, 2, P, PACK], BF16) for u in range(2)] for a in range(PASSES)]
+        xr_codes = [[sbuf("xr_codes%d_%d" % (a, u), [P, 2 * P], U32) for u in range(2)] for a in range(PASSES)]
+        xr_scales = [[sbuf("xr_scales%d_%d" % (a, u), [P, 2 * P], U8) for u in range(2)] for a in range(PASSES)]
+        acc = [[psum.tile([P, N_TILE], F32, name="acc%d_%d" % (h, r)) for r in range(PACK)] for h in range(HALVES)]
+        y = [sbuf("y%d" % h, [P, PACK, N_TILE], F32) for h in range(HALVES)]
+        y_bf0 = sbuf("y_bf0", [P, N_TILE, PACK], BF16)
+        y_bf1 = [sbuf("y_bf1_%d" % c, [P, N_TILE // 2, PACK], BF16) for c in range(2)]
+        y_codes = sbuf("y_codes", [P, M], U32)
+        y_scales = sbuf("y_scales", [P, M], U8)
+
+        out_rows = out_0.rearrange("(p r) n -> p r n", r=PACK)
+        out_words = out_1[0].rearrange("p n i -> p (n i)").bitcast(I32)
+
+        def load_scales(queue, plane, scales, q):
+            queue.dma_start(
+                out=plane[32 * q : 32 * q + 4, :, :].bitcast(I32),
+                in_=scales[:, 4 * q : 4 * q + 4, :].rearrange("a r n -> r a n").bitcast(I32),
+            )
+
+        def deal_scales(a):
+            nc.vector.tensor_copy(
+                out=xs[a][:].rearrange("p r (c m) -> p c r m", m=16),
+                in_=xs_raw[:, a, :].rearrange("p (c m r) -> p c r m", m=16, r=PACK),
+            )
+
+        def deal_words(a):
+            nc.vector.tensor_copy(
+                out=xw[a][:].rearrange("p r (c m b) -> p c r m b", m=8, b=2),
+                in_=xw_raw[a].rearrange("p (c m r b) -> p c r m b", m=8, r=PACK, b=2),
+            )
+
+        def round_xr(a, u):
+            src = xr_raw[a][:].rearrange("p j (m r) -> p m j r", r=PACK)[:, :, :, 2 * u : 2 * u + 2]
+            dst = xr_bf[a][u][:].rearrange("p r m j -> p m j r")
+            if u == 0:
+                nc.vector.tensor_copy(out=dst, in_=src)
+            else:
+                nc.scalar.copy(out=dst, in_=src)
+
+        def quantize_xr(a, u):
+            nc.vector.quantize_mx(
+                out=xr_codes[a][u][:].bitcast(FP8X4),
+                scales=xr_scales[a][u][:],
+                in_=xr_bf[a][u][:].rearrange("p r m j -> p (r m j)"),
+            )
+
+        def mm(lhsT, lhsT_scale, a, h, r, start, stop):
+            nc.tensor.matmul_mx(
+                out=acc[h][r][:],
+                lhsT=lhsT,
+                lhsT_scale=lhsT_scale,
+                rhs=ww[a][:, 2 * N_TILE * h : 2 * N_TILE * (h + 1)].bitcast(FP4X4),
+                rhs_scale=ws[:, a, N_TILE * h : N_TILE * (h + 1)],
+                start=start,
+                stop=stop,
+            )
+
+        def mm_x4(a, h, r):
+            mm(xw[a][:, r, :].bitcast(FP4X4), xs[a][:, r, :], a, h, r, a == 0, False)
+
+        def mm_xr(a, h, r):
+            cols = slice(P * (r % 2), P * (r % 2 + 1))
+            mm(xr_codes[a][r // 2][:, cols].bitcast(FP8X4), xr_scales[a][r // 2][:, cols], a, h, r, False, a == PASSES - 1)
+
+        def store_rows(h, r):
+            nc.sync.dma_start(out=out_rows[:, r, N_TILE * h : N_TILE * (h + 1)], in_=y[h][:, r, :])
+
+        def interleave(copy, dst, h, n0, n1):
+            copy(
+                out=dst.rearrange("p (c i) r -> p c r i", i=4),
+                in_=y[h][:, :, n0:n1].rearrange("p r (c i) -> p c r i", i=4),
+            )
+
+        def quantize_y(src, n0, n1):
+            nc.vector.quantize_mx(
+                out=y_codes[:, n0:n1].bitcast(FP8X4),
+                scales=y_scales[:, n0:n1],
+                in_=src.rearrange("p n r -> p (n r)"),
+            )
+
+        def store_codes(n0, n1):
+            nc.sync.dma_start(out=out_words[:, n0:n1], in_=y_codes[:, n0:n1].bitcast(I32))
+
+        nc.vector.memset(xs_raw[:].rearrange("p a t -> p (a t)").bitcast(I32), 0)
+        nc.vector.memset(ws[:].rearrange("p a n -> p (a n)").bitcast(I32), 0)
+        nc.sync.dma_start(out=xw_first[:], in_=x4_words[0])
+        for q in range(QUADS):
+            load_scales(nc.sync, xs_raw, x4_scales, q)
+        for q in range(QUADS - 1):
+            load_scales(nc.scalar, ws, w4_scales, q)
+        load_scales(nc.sync, ws, w4_scales, QUADS - 1)
+        nc.sync.dma_start(out=ww[0][:], in_=w4_words[0])
+        nc.sync.dma_start(out=ww[1][:], in_=w4_words[1])
+        nc.sync.dma_start(out=xw_rest[:], in_=x4_words[1:PASSES].rearrange("a p b -> p a b"))
+        xr_rows = xr.rearrange("(a p j) t -> a p j t", p=P, j=PACK)
+        nc.sync.dma_start(out=xr_raw[0][:], in_=xr_rows[0])
+        nc.sync.dma_start(out=ww[2][:], in_=w4_words[2])
+        nc.sync.dma_start(out=xr_raw[1][:], in_=xr_rows[1])
+        nc.sync.dma_start(out=xr_raw[2][:], in_=xr_rows[2])
+
+        for a in range(PASSES):
+            deal_scales(a)
+            deal_words(a)
+        for a in range(PASSES):
+            round_xr(a, 0)
+            round_xr(a, 1)
+            quantize_xr(a, 0)
+            quantize_xr(a, 1)
+
+        for a in range(PASSES - 1):
+            for r in range(PACK):
+                for h in range(HALVES):
+                    mm_x4(a, h, r)
+        for r in range(PACK):
+            for h in range(HALVES):
+                mm_xr(0, h, r)
+        for r in range(PACK):
+            mm_x4(2, 0, r)
+        for a in range(1, PASSES):
+            for r in range(PACK):
+                mm_xr(a, 0, r)
+        for r in range(PACK):
+            mm_x4(2, 1, r)
+            mm_xr(1, 1, r)
+            mm_xr(2, 1, r)
+
+        for r in range(PACK):
+            if r % 2 == 0:
+                nc.scalar.copy(out=y[0][:, r, :], in_=acc[0][r][:])
+            else:
+                nc.vector.tensor_copy(out=y[0][:, r, :], in_=acc[0][r][:])
+            store_rows(0, r)
+        interleave(nc.vector.tensor_copy, y_bf0[:], 0, 0, N_TILE)
+        quantize_y(y_bf0[:], 0, N_TILE)
+        for r in range(PACK - 1):
+            nc.scalar.copy(out=y[1][:, r, :], in_=acc[1][r][:])
+            store_rows(1, r)
+            if r == 1:
+                store_codes(0, N_TILE)
+        half = N_TILE // 2
+        quarter = N_TILE // 4
+        nc.scalar.copy(out=y[1][:, PACK - 1, :half], in_=acc[1][PACK - 1][:, :half])
+        nc.scalar.copy(out=y[1][:, PACK - 1, half:], in_=acc[1][PACK - 1][:, half:])
+        store_rows(1, PACK - 1)
+        interleave(nc.vector.tensor_copy, y_bf1[0][:], 1, 0, half)
+        interleave(nc.vector.tensor_copy, y_bf1[1][:, :quarter, :], 1, half, half + quarter)
+        interleave(nc.scalar.copy, y_bf1[1][:, quarter:, :], 1, half + quarter, N_TILE)
+        quantize_y(y_bf1[0][:], N_TILE, N_TILE + half)
+        store_codes(N_TILE, N_TILE + half)
+        quantize_y(y_bf1[1][:], N_TILE + half, M)
+        store_codes(N_TILE + half, M)
+        for q in range(QUADS):
+            queue = nc.scalar if q % 2 == 0 else nc.sync
+            queue.dma_start(
+                out=out_2[0, 4 * q : 4 * q + 4, :].bitcast(I32),
+                in_=y_scales[32 * q : 32 * q + 4, :].bitcast(I32),
+            )

@@ -38,7 +38,12 @@ def tile_mix_xres_tm_pl_none_kernel(
         xw_first = sbuf("xw_first", [P, 2 * T], U8)
         xw_rest = sbuf("xw_rest", [P, PASSES - 1, 2 * T], U8)
         xw_raw = [xw_first[:]] + [xw_rest[:, a, :] for a in range(PASSES - 1)]
-        ww = [sbuf("ww%d" % a, [P, 2 * M], U8) for a in range(PASSES)]
+        ww_mid = sbuf("ww_mid", [P, HALVES, 2 * N_TILE], U8)
+        ww = [
+            [sbuf("ww0_%d" % h, [P, 2 * N_TILE], U8)[:] for h in range(HALVES)],
+            [ww_mid[:, h, :] for h in range(HALVES)],
+            [sbuf("ww2_%d" % h, [P, 2 * N_TILE], U8)[:] for h in range(HALVES)],
+        ]
         xw = [sbuf("xw%d" % a, [P, PACK, 2 * P], U8) for a in range(PASSES)]
         xs = [sbuf("xs%d" % a, [P, PACK, P], U8) for a in range(PASSES)]
         xr_raw = [sbuf("xr_raw%d" % a, [P, PACK, T], F32) for a in range(PASSES)]
@@ -57,8 +62,8 @@ def tile_mix_xres_tm_pl_none_kernel(
 
         def load_scales(queue, plane, scales, q):
             queue.dma_start(
-                out=plane[32 * q : 32 * q + 4, :, :].bitcast(I32),
-                in_=scales[:, 4 * q : 4 * q + 4, :].rearrange("a r n -> r a n").bitcast(I32),
+                out=plane[q:P:32, :, :].bitcast(I32),
+                in_=scales.rearrange("a (g r) n -> r g a n", r=4)[q].bitcast(I32),
             )
 
         def deal_scales(a):
@@ -81,11 +86,11 @@ def tile_mix_xres_tm_pl_none_kernel(
             else:
                 nc.scalar.copy(out=dst, in_=src)
 
-        def quantize_xr(a, u):
+        def quantize_xr(a, u, r0, r1):
             nc.vector.quantize_mx(
-                out=xr_codes[a][u][:].bitcast(FP8X4),
-                scales=xr_scales[a][u][:],
-                in_=xr_bf[a][u][:].rearrange("p r m j -> p (r m j)"),
+                out=xr_codes[a][u][:, P * r0 : P * r1].bitcast(FP8X4),
+                scales=xr_scales[a][u][:, P * r0 : P * r1],
+                in_=xr_bf[a][u][:, r0:r1].rearrange("p r m j -> p (r m j)"),
             )
 
         def mm(lhsT, lhsT_scale, a, h, r, start, stop):
@@ -93,18 +98,22 @@ def tile_mix_xres_tm_pl_none_kernel(
                 out=acc[h][r][:],
                 lhsT=lhsT,
                 lhsT_scale=lhsT_scale,
-                rhs=ww[a][:, 2 * N_TILE * h : 2 * N_TILE * (h + 1)].bitcast(FP4X4),
+                rhs=ww[a][h].bitcast(FP4X4),
                 rhs_scale=ws[:, a, N_TILE * h : N_TILE * (h + 1)],
                 start=start,
                 stop=stop,
             )
 
-        def mm_x4(a, h, r):
+        def x4_pass(a, h, r):
             mm(xw[a][:, r, :].bitcast(FP4X4), xs[a][:, r, :], a, h, r, a == 0, False)
 
-        def mm_xr(a, h, r):
+        def xr_pass(a, h, r):
             cols = slice(P * (r % 2), P * (r % 2 + 1))
             mm(xr_codes[a][r // 2][:, cols].bitcast(FP8X4), xr_scales[a][r // 2][:, cols], a, h, r, False, a == PASSES - 1)
+
+        half = N_TILE // 2
+        quarter = N_TILE // 4
+        last = PACK - 1
 
         def store_rows(h, r):
             nc.sync.dma_start(out=out_rows[:, r, N_TILE * h : N_TILE * (h + 1)], in_=y[h][:, r, :])
@@ -128,45 +137,57 @@ def tile_mix_xres_tm_pl_none_kernel(
         nc.vector.memset(xs_raw[:].rearrange("p a t -> p (a t)").bitcast(I32), 0)
         nc.vector.memset(ws[:].rearrange("p a n -> p (a n)").bitcast(I32), 0)
         nc.sync.dma_start(out=xw_first[:], in_=x4_words[0])
+        nc.sync.dma_start(out=ww[0][0], in_=w4_words[0][:, : 2 * N_TILE])
         for q in range(QUADS):
             load_scales(nc.sync, xs_raw, x4_scales, q)
-        for q in range(QUADS - 1):
-            load_scales(nc.scalar, ws, w4_scales, q)
-        load_scales(nc.sync, ws, w4_scales, QUADS - 1)
-        nc.sync.dma_start(out=ww[0][:], in_=w4_words[0])
-        nc.sync.dma_start(out=ww[1][:], in_=w4_words[1])
+        for q in range(QUADS):
+            load_scales(nc.scalar if q < 2 else nc.sync, ws, w4_scales, q)
+        nc.sync.dma_start(out=ww[0][1], in_=w4_words[0][:, 2 * N_TILE :])
         nc.sync.dma_start(out=xw_rest[:], in_=x4_words[1:PASSES].rearrange("a p b -> p a b"))
+        nc.sync.dma_start(out=ww_mid[:].rearrange("p h b -> p (h b)"), in_=w4_words[1])
         xr_rows = xr.rearrange("(a p j) t -> a p j t", p=P, j=PACK)
         nc.sync.dma_start(out=xr_raw[0][:], in_=xr_rows[0])
-        nc.sync.dma_start(out=ww[2][:], in_=w4_words[2])
+        nc.sync.dma_start(out=ww[2][0], in_=w4_words[2][:, : 2 * N_TILE])
         nc.sync.dma_start(out=xr_raw[1][:], in_=xr_rows[1])
         nc.sync.dma_start(out=xr_raw[2][:], in_=xr_rows[2])
+        nc.sync.dma_start(out=ww[2][1], in_=w4_words[2][:, 2 * N_TILE :])
 
         for a in range(PASSES):
-            deal_scales(a)
             deal_words(a)
+            deal_scales(a)
         for a in range(PASSES):
             round_xr(a, 0)
             round_xr(a, 1)
-            quantize_xr(a, 0)
-            quantize_xr(a, 1)
+            quantize_xr(a, 0, 0, 1)
+            quantize_xr(a, 0, 1, 2)
+            quantize_xr(a, 1, 0, 2)
 
+        for i in range(3):
+            nc.tensor.matmul_mx(
+                out=acc[1][last][:],
+                lhsT=xw_first[:, : 2 * P].bitcast(FP4X4),
+                lhsT_scale=xs_raw[:, 0, :P],
+                rhs=xw_first[:].bitcast(FP4X4),
+                rhs_scale=xs_raw[:, 0, :],
+                start=True,
+                stop=True,
+            )
         for a in range(PASSES - 1):
-            for r in range(PACK):
-                for h in range(HALVES):
-                    mm_x4(a, h, r)
-        for r in range(PACK):
             for h in range(HALVES):
-                mm_xr(0, h, r)
+                for r in range(PACK):
+                    x4_pass(a, h, r)
+        for h in range(HALVES):
+            for r in range(PACK):
+                xr_pass(0, h, r)
         for r in range(PACK):
-            mm_x4(2, 0, r)
+            x4_pass(2, 0, r)
         for a in range(1, PASSES):
             for r in range(PACK):
-                mm_xr(a, 0, r)
+                xr_pass(a, 0, r)
         for r in range(PACK):
-            mm_x4(2, 1, r)
-            mm_xr(1, 1, r)
-            mm_xr(2, 1, r)
+            x4_pass(2, 1, r)
+            xr_pass(1, 1, r)
+            xr_pass(2, 1, r)
 
         for r in range(PACK):
             if r % 2 == 0:
@@ -174,6 +195,7 @@ def tile_mix_xres_tm_pl_none_kernel(
             else:
                 nc.vector.tensor_copy(out=y[0][:, r, :], in_=acc[0][r][:])
             store_rows(0, r)
+
         interleave(nc.vector.tensor_copy, y_bf0[:], 0, 0, N_TILE)
         quantize_y(y_bf0[:], 0, N_TILE)
         for r in range(PACK - 1):
@@ -181,12 +203,10 @@ def tile_mix_xres_tm_pl_none_kernel(
             store_rows(1, r)
             if r == 1:
                 store_codes(0, N_TILE)
-        half = N_TILE // 2
-        quarter = N_TILE // 4
-        nc.scalar.copy(out=y[1][:, PACK - 1, :half], in_=acc[1][PACK - 1][:, :half])
-        nc.scalar.copy(out=y[1][:, PACK - 1, half:], in_=acc[1][PACK - 1][:, half:])
-        store_rows(1, PACK - 1)
+        nc.scalar.copy(out=y[1][:, last, :half], in_=acc[1][last][:, :half])
         interleave(nc.vector.tensor_copy, y_bf1[0][:], 1, 0, half)
+        nc.scalar.copy(out=y[1][:, last, half:], in_=acc[1][last][:, half:])
+        store_rows(1, last)
         interleave(nc.vector.tensor_copy, y_bf1[1][:, :quarter, :], 1, half, half + quarter)
         interleave(nc.scalar.copy, y_bf1[1][:, quarter:, :], 1, half + quarter, N_TILE)
         quantize_y(y_bf1[0][:], N_TILE, N_TILE + half)

@@ -38,12 +38,9 @@ def tile_mix_xres_tm_pl_none_kernel(
         xw_first = sbuf("xw_first", [P, 2 * T], U8)
         xw_rest = sbuf("xw_rest", [P, PASSES - 1, 2 * T], U8)
         xw_raw = [xw_first[:]] + [xw_rest[:, a, :] for a in range(PASSES - 1)]
-        ww_mid = sbuf("ww_mid", [P, HALVES, 2 * N_TILE], U8)
-        ww = [
-            [sbuf("ww0_%d" % h, [P, 2 * N_TILE], U8)[:] for h in range(HALVES)],
-            [ww_mid[:, h, :] for h in range(HALVES)],
-            [sbuf("ww2_%d" % h, [P, 2 * N_TILE], U8)[:] for h in range(HALVES)],
-        ]
+        ww_whole = [sbuf("ww%d" % a, [P, HALVES, 2 * N_TILE], U8) for a in range(PASSES - 1)]
+        ww = [[tile[:, h, :] for h in range(HALVES)] for tile in ww_whole]
+        ww.append([sbuf("ww_last%d" % h, [P, 2 * N_TILE], U8)[:] for h in range(HALVES)])
         xw = [sbuf("xw%d" % a, [P, PACK, 2 * P], U8) for a in range(PASSES)]
         xs = [sbuf("xs%d" % a, [P, PACK, P], U8) for a in range(PASSES)]
         xr_raw = [sbuf("xr_raw%d" % a, [P, PACK, T], F32) for a in range(PASSES)]
@@ -62,8 +59,8 @@ def tile_mix_xres_tm_pl_none_kernel(
 
         def load_scales(queue, plane, scales, q):
             queue.dma_start(
-                out=plane[q:P:32, :, :].bitcast(I32),
-                in_=scales.rearrange("a (g r) n -> r g a n", r=4)[q].bitcast(I32),
+                out=plane[32 * q : 32 * q + 4, :, :].bitcast(I32),
+                in_=scales[:, 4 * q : 4 * q + 4, :].rearrange("a r n -> r a n").bitcast(I32),
             )
 
         def deal_scales(a):
@@ -134,17 +131,24 @@ def tile_mix_xres_tm_pl_none_kernel(
         def store_codes(n0, n1):
             nc.sync.dma_start(out=out_words[:, n0:n1], in_=y_codes[:, n0:n1].bitcast(I32))
 
+        def store_scales(queues, n0, n1):
+            for q in range(QUADS):
+                queues[q % len(queues)].dma_start(
+                    out=out_2[0, 4 * q : 4 * q + 4, n0:n1].bitcast(I32),
+                    in_=y_scales[32 * q : 32 * q + 4, n0:n1].bitcast(I32),
+                )
+
         nc.vector.memset(xs_raw[:].rearrange("p a t -> p (a t)").bitcast(I32), 0)
         nc.vector.memset(ws[:].rearrange("p a n -> p (a n)").bitcast(I32), 0)
         nc.sync.dma_start(out=xw_first[:], in_=x4_words[0])
-        nc.sync.dma_start(out=ww[0][0], in_=w4_words[0][:, : 2 * N_TILE])
         for q in range(QUADS):
             load_scales(nc.sync, xs_raw, x4_scales, q)
-        for q in range(QUADS):
-            load_scales(nc.scalar if q < 2 else nc.sync, ws, w4_scales, q)
-        nc.sync.dma_start(out=ww[0][1], in_=w4_words[0][:, 2 * N_TILE :])
+        for q in range(QUADS - 1):
+            load_scales(nc.scalar, ws, w4_scales, q)
+        load_scales(nc.sync, ws, w4_scales, QUADS - 1)
+        for a in range(PASSES - 1):
+            nc.sync.dma_start(out=ww_whole[a][:].rearrange("p h b -> p (h b)"), in_=w4_words[a])
         nc.sync.dma_start(out=xw_rest[:], in_=x4_words[1:PASSES].rearrange("a p b -> p a b"))
-        nc.sync.dma_start(out=ww_mid[:].rearrange("p h b -> p (h b)"), in_=w4_words[1])
         xr_rows = xr.rearrange("(a p j) t -> a p j t", p=P, j=PACK)
         nc.sync.dma_start(out=xr_raw[0][:], in_=xr_rows[0])
         nc.sync.dma_start(out=ww[2][0], in_=w4_words[2][:, : 2 * N_TILE])
@@ -162,22 +166,12 @@ def tile_mix_xres_tm_pl_none_kernel(
             quantize_xr(a, 0, 1, 2)
             quantize_xr(a, 1, 0, 2)
 
-        for i in range(3):
-            nc.tensor.matmul_mx(
-                out=acc[1][last][:],
-                lhsT=xw_first[:, : 2 * P].bitcast(FP4X4),
-                lhsT_scale=xs_raw[:, 0, :P],
-                rhs=xw_first[:].bitcast(FP4X4),
-                rhs_scale=xs_raw[:, 0, :],
-                start=True,
-                stop=True,
-            )
         for a in range(PASSES - 1):
-            for h in range(HALVES):
-                for r in range(PACK):
-                    x4_pass(a, h, r)
-        for h in range(HALVES):
             for r in range(PACK):
+                for h in range(HALVES):
+                    x4_pass(a, h, r)
+        for r in range(PACK):
+            for h in range(HALVES):
                 xr_pass(0, h, r)
         for r in range(PACK):
             x4_pass(2, 0, r)
@@ -189,7 +183,10 @@ def tile_mix_xres_tm_pl_none_kernel(
             xr_pass(1, 1, r)
             xr_pass(2, 1, r)
 
-        for r in range(PACK):
+        for n0 in (0, half):
+            nc.scalar.copy(out=y[0][:, 0, n0 : n0 + half], in_=acc[0][0][:, n0 : n0 + half])
+            nc.sync.dma_start(out=out_rows[:, 0, n0 : n0 + half], in_=y[0][:, 0, n0 : n0 + half])
+        for r in range(1, PACK):
             if r % 2 == 0:
                 nc.scalar.copy(out=y[0][:, r, :], in_=acc[0][r][:])
             else:
@@ -213,9 +210,4 @@ def tile_mix_xres_tm_pl_none_kernel(
         store_codes(N_TILE, N_TILE + half)
         quantize_y(y_bf1[1][:], N_TILE + half, M)
         store_codes(N_TILE + half, M)
-        for q in range(QUADS):
-            queue = nc.scalar if q % 2 == 0 else nc.sync
-            queue.dma_start(
-                out=out_2[0, 4 * q : 4 * q + 4, :].bitcast(I32),
-                in_=y_scales[32 * q : 32 * q + 4, :].bitcast(I32),
-            )
+        store_scales([nc.scalar, nc.sync], 0, M)

from contextlib import ExitStack

import concourse.mybir as mybir

K, M, T = 1536, 1024, 512
FLOPS = 2 * 2 * K * M * T

F32 = mybir.dt.float32
BF16 = mybir.dt.bfloat16
I32 = mybir.dt.int32
U32 = mybir.dt.uint32
U8 = mybir.dt.uint8
FP8X4 = mybir.dt.float8_e4m3fn_x4
FP4X4 = mybir.dt.float4_e2m1fn_x4

P = 128
PACK = 4
PASSES = K // (P * PACK)
N_TILE = 512
HALVES = M // N_TILE
QUADS = 4


def tile_mix_xres_tm_pl_none_kernel(
    tc, x4_words, x4_scales, xr, w4_words, w4_scales, out_0, out_1, out_2
):
    nc = tc.nc
    with ExitStack() as ctx:
        sb = ctx.enter_context(tc.tile_pool(name="sb", bufs=1))
        psum = ctx.enter_context(tc.psum_pool(name="psum", bufs=1))
        ctx.enter_context(tc.manual_schedule())

        def sbuf(name, shape, dtype):
            return sb.tile(shape, dtype, name=name, align_bytes=64)

        xs_raw = sbuf("xs_raw", [P, PASSES, T], U8)
        ws = sbuf("ws", [P, PASSES, M], U8)
        xw_first = sbuf("xw_first", [P, 2 * T], U8)
        xw_rest = sbuf("xw_rest", [P, PASSES - 1, 2 * T], U8)
        xw_raw = [xw_first[:]] + [xw_rest[:, a, :] for a in range(PASSES - 1)]
        ww_whole = [sbuf("ww%d" % a, [P, HALVES, 2 * N_TILE], U8) for a in range(PASSES - 1)]
        ww = [[tile[:, h, :] for h in range(HALVES)] for tile in ww_whole]
        ww.append([sbuf("ww_last%d" % h, [P, 2 * N_TILE], U8)[:] for h in range(HALVES)])
        xw = [sbuf("xw%d" % a, [P, PACK, 2 * P], U8) for a in range(PASSES)]
        xs = [sbuf("xs%d" % a, [P, PACK, P], U8) for a in range(PASSES)]
        xr_raw = [sbuf("xr_raw%d" % a, [P, PACK, T], F32) for a in range(PASSES)]
        xr_bf = [[sbuf("xr_bf%d_%d" % (a, u), [P, 2, P, PACK], BF16) for u in range(2)] for a in range(PASSES)]
        xr_codes = [[sbuf("xr_codes%d_%d" % (a, u), [P, 2 * P], U32) for u in range(2)] for a in range(PASSES)]
        xr_scales = [[sbuf("xr_scales%d_%d" % (a, u), [P, 2 * P], U8) for u in range(2)] for a in range(PASSES)]
        acc = [[psum.tile([P, N_TILE], F32, name="acc%d_%d" % (h, r)) for r in range(PACK)] for h in range(HALVES)]
        y = [sbuf("y%d" % h, [P, PACK, N_TILE], F32) for h in range(HALVES)]
        y_bf0 = sbuf("y_bf0", [P, N_TILE, PACK], BF16)
        y_bf1 = [sbuf("y_bf1_%d" % c, [P, N_TILE // 2, PACK], BF16) for c in range(2)]
        y_codes = sbuf("y_codes", [P, M], U32)
        y_scales = sbuf("y_scales", [P, M], U8)

        out_rows = out_0.rearrange("(p r) n -> p r n", r=PACK)
        out_words = out_1[0].rearrange("p n i -> p (n i)").bitcast(I32)

        def load_scales(queue, plane, scales, q):
            queue.dma_start(
                out=plane[32 * q : 32 * q + 4, :, :].bitcast(I32),
                in_=scales[:, 4 * q : 4 * q + 4, :].rearrange("a r n -> r a n").bitcast(I32),
            )

        def deal_scales(a):
            nc.vector.tensor_copy(
                out=xs[a][:].rearrange("p r (c m) -> p c r m", m=16),
                in_=xs_raw[:, a, :].rearrange("p (c m r) -> p c r m", m=16, r=PACK),
            )

        def deal_words(a):
            nc.vector.tensor_copy(
                out=xw[a][:].rearrange("p r (c m b) -> p c r m b", m=8, b=2),
                in_=xw_raw[a].rearrange("p (c m r b) -> p c r m b", m=8, r=PACK, b=2),
            )

        def round_xr(a, u):
            src = xr_raw[a][:].rearrange("p j (m r) -> p m j r", r=PACK)[:, :, :, 2 * u : 2 * u + 2]
            dst = xr_bf[a][u][:].rearrange("p r m j -> p m j r")
            if u == 0:
                nc.vector.tensor_copy(out=dst, in_=src)
            else:
                nc.scalar.copy(out=dst, in_=src)

        def quantize_xr(a, u, r0, r1):
            nc.vector.quantize_mx(
                out=xr_codes[a][u][:, P * r0 : P * r1].bitcast(FP8X4),
                scales=xr_scales[a][u][:, P * r0 : P * r1],
                in_=xr_bf[a][u][:, r0:r1].rearrange("p r m j -> p (r m j)"),
            )

        def mm(lhsT, lhsT_scale, a, h, r, start, stop):
            nc.tensor.matmul_mx(
                out=acc[h][r][:],
                lhsT=lhsT,
                lhsT_scale=lhsT_scale,
                rhs=ww[a][h].bitcast(FP4X4),
                rhs_scale=ws[:, a, N_TILE * h : N_TILE * (h + 1)],
                start=start,
                stop=stop,
            )

        def x4_pass(a, h, r):
            mm(xw[a][:, r, :].bitcast(FP4X4), xs[a][:, r, :], a, h, r, a == 0, False)

        def xr_pass(a, h, r):
            cols = slice(P * (r % 2), P * (r % 2 + 1))
            mm(xr_codes[a][r // 2][:, cols].bitcast(FP8X4), xr_scales[a][r // 2][:, cols], a, h, r, False, a == PASSES - 1)

        half = N_TILE // 2
        quarter = N_TILE // 4
        last = PACK - 1

        def store_rows(h, r):
            nc.sync.dma_start(out=out_rows[:, r, N_TILE * h : N_TILE * (h + 1)], in_=y[h][:, r, :])

        def interleave(copy, dst, h, n0, n1):
            copy(
                out=dst.rearrange("p (c i) r -> p c r i", i=4),
                in_=y[h][:, :, n0:n1].rearrange("p r (c i) -> p c r i", i=4),
            )

        def quantize_y(src, n0, n1):
            nc.vector.quantize_mx(
                out=y_codes[:, n0:n1].bitcast(FP8X4),
                scales=y_scales[:, n0:n1],
                in_=src.rearrange("p n r -> p (n r)"),
            )

        def store_codes(n0, n1):
            nc.sync.dma_start(out=out_words[:, n0:n1], in_=y_codes[:, n0:n1].bitcast(I32))

        def store_scales(queues, n0, n1):
            for q in range(QUADS):
                queues[q % len(queues)].dma_start(
                    out=out_2[0, 4 * q : 4 * q + 4, n0:n1].bitcast(I32),
                    in_=y_scales[32 * q : 32 * q + 4, n0:n1].bitcast(I32),
                )

        nc.vector.memset(xs_raw[:].rearrange("p a t -> p (a t)").bitcast(I32), 0)
        nc.vector.memset(ws[:].rearrange("p a n -> p (a n)").bitcast(I32), 0)
        nc.sync.dma_start(out=xw_first[:], in_=x4_words[0])
        for q in range(QUADS):
            load_scales(nc.sync, xs_raw, x4_scales, q)
        for q in range(QUADS - 1):
            load_scales(nc.scalar, ws, w4_scales, q)
        load_scales(nc.sync, ws, w4_scales, QUADS - 1)
        for a in range(PASSES - 1):
            nc.sync.dma_start(out=ww_whole[a][:].rearrange("p h b -> p (h b)"), in_=w4_words[a])
        nc.sync.dma_start(out=xw_rest[:], in_=x4_words[1:PASSES].rearrange("a p b -> p a b"))
        xr_rows = xr.rearrange("(a p j) t -> a p j t", p=P, j=PACK)
        nc.sync.dma_start(out=xr_raw[0][:], in_=xr_rows[0])
        nc.sync.dma_start(out=ww[2][0], in_=w4_words[2][:, : 2 * N_TILE])
        nc.sync.dma_start(out=xr_raw[1][:], in_=xr_rows[1])
        nc.sync.dma_start(out=xr_raw[2][:], in_=xr_rows[2])
        nc.sync.dma_start(out=ww[2][1], in_=w4_words[2][:, 2 * N_TILE :])

        for a in range(PASSES):
            deal_words(a)
            deal_scales(a)
        for a in range(PASSES):
            round_xr(a, 0)
            round_xr(a, 1)
            quantize_xr(a, 0, 0, 1)
            quantize_xr(a, 0, 1, 2)
            quantize_xr(a, 1, 0, 2)

        for a in range(PASSES - 1):
            for r in range(PACK):
                for h in range(HALVES):
                    x4_pass(a, h, r)
        for r in range(PACK):
            for h in range(HALVES):
                xr_pass(0, h, r)
        for r in range(PACK):
            x4_pass(2, 0, r)
        for a in range(1, PASSES):
            for r in range(PACK):
                xr_pass(a, 0, r)
        for r in range(PACK):
            x4_pass(2, 1, r)
            xr_pass(1, 1, r)
            xr_pass(2, 1, r)

        for n0 in (0, half):
            nc.scalar.copy(out=y[0][:, 0, n0 : n0 + half], in_=acc[0][0][:, n0 : n0 + half])
            nc.sync.dma_start(out=out_rows[:, 0, n0 : n0 + half], in_=y[0][:, 0, n0 : n0 + half])
        for r in range(1, PACK):
            if r % 2 == 0:
                nc.scalar.copy(out=y[0][:, r, :], in_=acc[0][r][:])
            else:
                nc.vector.tensor_copy(out=y[0][:, r, :], in_=acc[0][r][:])
            store_rows(0, r)

        interleave(nc.vector.tensor_copy, y_bf0[:], 0, 0, N_TILE)
        quantize_y(y_bf0[:], 0, N_TILE)
        for r in range(PACK - 1):
            nc.scalar.copy(out=y[1][:, r, :], in_=acc[1][r][:])
            store_rows(1, r)
            if r == 1:
                store_codes(0, N_TILE)
        nc.scalar.copy(out=y[1][:, last, :half], in_=acc[1][last][:, :half])
        interleave(nc.vector.tensor_copy, y_bf1[0][:], 1, 0, half)
        nc.scalar.copy(out=y[1][:, last, half:], in_=acc[1][last][:, half:])
        store_rows(1, last)
        interleave(nc.vector.tensor_copy, y_bf1[1][:, :quarter, :], 1, half, half + quarter)
        interleave(nc.scalar.copy, y_bf1[1][:, quarter:, :], 1, half + quarter, N_TILE)
        quantize_y(y_bf1[0][:], N_TILE, N_TILE + half)
        store_codes(N_TILE, N_TILE + half)
        quantize_y(y_bf1[1][:], N_TILE + half, M)
        store_codes(N_TILE + half, M)
        store_scales([nc.scalar, nc.sync], 0, M)
